import numpy as np, ml_dtypes
CORES = [35,38,43,46]
N = 4
R = 512
def setup_inputs(rng):
    m = (rng.standard_normal((N, 128, 128), dtype=np.float32) / 11).astype(ml_dtypes.bfloat16)
    q = rng.standard_normal((128, R), dtype=np.float32).astype(ml_dtypes.bfloat16)
    return {"m": m, "mt": m.transpose(0, 2, 1).copy(), "q": np.broadcast_to(q, (N, 128, R)).copy()}
def setup_inputs_big(rng):
    d = setup_inputs(rng)
    for k in ("m", "mt", "q"): d[k] = (d[k].astype(np.float32) * 1024.0).astype(d[k].dtype)
    return d
def setup_inputs_small(rng):
    d = setup_inputs(rng)
    for k in ("m", "mt", "q"): d[k] = (d[k].astype(np.float32) * (1 / 1024.0)).astype(d[k].dtype)
    return d
def setup_inputs_apart(rng):
    d = setup_inputs(rng)
    f = (10.0 ** rng.permutation(np.linspace(-1.5, 1.5, N))).astype(np.float32).reshape(N, 1, 1)
    for k in ("m", "mt"): d[k] = (d[k].astype(np.float32) * f).astype(d[k].dtype)
    return d
def tie_inputs(x):
    x = dict(x)
    x["mt"] = x["m"].transpose(0, 2, 1).copy(); x["q"] = np.broadcast_to(x["q"][0], x["q"].shape).copy()
    return x
def reference(m, mt, q):
    M, MT, Q = m.astype(np.float64), mt.astype(np.float64), q.astype(np.float64)
    p = sum(MT[j].T @ Q[j] for j in range(N))
    q2 = sum(M[j].T @ p for j in range(N))
    return {"p": np.broadcast_to(p.astype(ml_dtypes.bfloat16 if m.dtype != np.float64 else np.float64), (N, 128, R)), "q2": np.broadcast_to(q2.astype(ml_dtypes.bfloat16 if m.dtype != np.float64 else np.float64), (N, 128, R))}

@@ -1,0 +1,155 @@
+from concourse.bass import DstId, RemoteDMATransfer
+from concourse.mybir import AluOpType
+
+D = 128
+R = 512
+H = R // 2
+BITS = 7
+
+SCRATCH = {
+    "land": ("sbuf", [128, 4 * D], "bfloat16"),
+    "qs": ("sbuf", [128, R], "bfloat16"),
+    "ones": ("sbuf", [128, D], "bfloat16"),
+    "neg6": ("sbuf", [128, D], "bfloat16"),
+    "zero": ("sbuf", [128, D], "bfloat16"),
+    "ident": ("sbuf", [128, D], "bfloat16"),
+    "s_bf": ("sbuf", [128, D], "bfloat16"),
+    "p_bf": ("sbuf", [128, R], "bfloat16"),
+    "q2_bf": ("sbuf", [128, R], "bfloat16"),
+    "ps_p0": ("psum", [128, 512], "float32"),
+    "ps_p1": ("psum", [128, 512], "float32"),
+    "ps_s": ("psum", [128, 512], "float32"),
+    "ps_q0": ("psum", [128, 512], "float32"),
+    "ps_q1": ("psum", [128, 512], "float32"),
+    "ps_c": ("psum", [128, 512], "float32"),
+}
+for _b in range(BITS):
+    SCRATCH["sg%d" % _b] = ("sbuf", [128, D >> (_b + 1), 2 << _b], "bfloat16")
+SEMAPHORES = ["ld_mt", "ld_q", "fill", "mm_c", "cp_id", "sent", "arr0", "arr1", "arr2", "arr3",
+              "mm_p0", "mm_p1", "mm_s", "mm_q0", "mm_q1", "cp_p0", "cp_p1", "cp_s", "cp_q0", "cp_q1",
+              "st_p0", "st_p1", "st_q0", "st_q1"]
+
+
+def _bits(mask):
+    return [b for b in range(mask.bit_length()) if (mask >> b) & 1]
+
+
+def _mask(bits):
+    m = 0
+    for b in bits:
+        m |= 1 << b
+    return m
+
+
+def _plan(src, cores, topo):
+    peers = [c for c in cores if c != src]
+    away = [c for c in peers if topo.chip(c) != topo.chip(src)]
+    near = [c for c in peers if topo.chip(c) == topo.chip(src)]
+    plan = {}
+    used = []
+    for k, c in enumerate(away):
+        e = _bits(topo.mask(src, c))
+        n = len(e) // len(away)
+        plan[c] = e[k * n:(k + 1) * n]
+        used += plan[c]
+    for c in near:
+        e = [b for b in _bits(topo.mask(src, c)) if b not in used]
+        plan[c] = e[:4]
+        used += plan[c]
+    return plan
+
+
+def rank_program(g, core, T, topo):
+    rank = T.rank_of(core)
+    if rank is None:
+        return
+    S = T.sem
+    cores = list(T.cores)
+    te = g.tensor
+    ve = g.vector
+
+    def slot(j):
+        return T.land[:, j * D:(j + 1) * D]
+
+    g.sync.dma_start(slot(rank), T.mt[:, :]).then_inc(S.ld_mt, 16)
+    g.sync.dma_start(T.qs[:, :], T.q[:, :]).then_inc(S.ld_q, 16)
+
+    fills = 0
+    for b in range(BITS):
+        w = 1 << b
+        ve.memset(T["sg%d" % b][0:1, :, 0:w], -1.0).then_inc(S.fill, 1)
+        ve.memset(T["sg%d" % b][0:1, :, w:2 * w], 1.0).then_inc(S.fill, 1)
+        fills += 2
+    ve.memset(T.ones[0:1, :], 1.0).then_inc(S.fill, 1)
+    ve.memset(T.neg6[0:1, :], -6.0).then_inc(S.fill, 1)
+    ve.memset(T.zero[:, :], 0.0).then_inc(S.fill, 1)
+    fills += 3
+    te.wait_ge(S.fill, fills)
+    for b in range(BITS):
+        row = T["sg%d" % b][0:1, :, :]
+        te.matmul(T.ps_c[:, 0:D], row, row, b == 0, False).then_inc(S.mm_c, 1)
+    te.matmul(T.ps_c[:, 0:D], T.ones[0:1, :], T.neg6[0:1, :], False, True).then_inc(S.mm_c, 1)
+    ve.wait_ge(S.fill, fills)
+    ve.wait_ge(S.mm_c, BITS + 1)
+    ve.tensor_tensor(T.ident[:, :], T.ps_c[:, 0:D], T.zero[:, :], AluOpType.max).then_inc(S.cp_id, 1)
+
+    plan = _plan(core, cores, topo)
+    transfers = []
+    total = 0
+    for dst, eng in plan.items():
+        rid, pid, _ = topo.addr(dst)
+        transfers.append(RemoteDMATransfer(dst_ids=[DstId(rid=rid, pnc=pid)], dma_engine_mask=_mask(eng),
+                                           remote_sem=S["arr%d" % rank], src=slot(rank), dst=slot(rank)))
+        total += len(eng)
+    g.wait_ge(S.ld_mt, 16)
+    g.remote_dma_fused(transfers, local_sem=S.sent)
+    g.wait_ge(S.sent, total)
+
+    def key(c):
+        return (c != core, topo.chip(c) != topo.chip(core), topo.die(c) != topo.die(core))
+    order = sorted(cores, key=key)
+    n = len(order)
+    te.wait_ge(S.ld_mt, 16)
+    te.wait_ge(S.ld_q, 16)
+    for k, c in enumerate(order):
+        j = T.rank_of(c)
+        if c != core:
+            te.wait_ge(S["arr%d" % j], len(_plan(c, cores, topo)[core]))
+        a, z = k == 0, k == n - 1
+        te.matmul(T.ps_p0[:, 0:H], slot(j), T.qs[:, 0:H], a, z).then_inc(S.mm_p0, 1)
+        if k == 0:
+            te.matmul(T.ps_p1[:, 0:H], slot(j), T.qs[:, H:R], a, z).then_inc(S.mm_p1, 1)
+            te.wait_ge(S.cp_id, 1)
+            te.matmul(T.ps_s[:, 0:D], slot(j), T.ident[:, :], a, z).then_inc(S.mm_s, 1)
+        else:
+            te.matmul(T.ps_s[:, 0:D], slot(j), T.ident[:, :], a, z).then_inc(S.mm_s, 1)
+            te.matmul(T.ps_p1[:, 0:H], slot(j), T.qs[:, H:R], a, z).then_inc(S.mm_p1, 1)
+    te.wait_ge(S.cp_p0, 1)
+    te.wait_ge(S.cp_s, 1)
+    te.matmul(T.ps_q0[:, 0:H], T.s_bf[:, :], T.p_bf[:, 0:H], True, True).then_inc(S.mm_q0, 1)
+    te.wait_ge(S.cp_p1, 1)
+    te.matmul(T.ps_q1[:, 0:H], T.s_bf[:, :], T.p_bf[:, H:R], True, True).then_inc(S.mm_q1, 1)
+
+    ve.wait_ge(S.mm_p0, n)
+    ve.tensor_copy(T.p_bf[:, 0:H], T.ps_p0[:, 0:H]).then_inc(S.cp_p0, 1)
+    ve.wait_ge(S.mm_s, n)
+    ve.tensor_copy(T.s_bf[:, :], T.ps_s[:, 0:D]).then_inc(S.cp_s, 1)
+    ve.wait_ge(S.mm_p1, n)
+    ve.tensor_copy(T.p_bf[:, H:R], T.ps_p1[:, 0:H]).then_inc(S.cp_p1, 1)
+    ve.wait_ge(S.mm_q0, 1)
+    ve.tensor_copy(T.q2_bf[:, 0:H], T.ps_q0[:, 0:H]).then_inc(S.cp_q0, 1)
+    ve.wait_ge(S.mm_q1, 1)
+    ve.tensor_copy(T.q2_bf[:, H:R], T.ps_q1[:, 0:H]).then_inc(S.cp_q1, 1)
+
+    g.sync.wait_ge(S.cp_p0, 1)
+    g.sync.dma_start(T.p[:, 0:H], T.p_bf[:, 0:H]).then_inc(S.st_p0, 16)
+    g.sync.wait_ge(S.cp_q0, 1)
+    g.sync.dma_start(T.q2[:, 0:H], T.q2_bf[:, 0:H]).then_inc(S.st_q0, 16)
+    g.scalar.wait_ge(S.cp_p1, 1)
+    g.scalar.dma_start(T.p[:, H:R], T.p_bf[:, H:R]).then_inc(S.st_p1, 16)
+    g.scalar.wait_ge(S.cp_q1, 1)
+    g.scalar.dma_start(T.q2[:, H:R], T.q2_bf[:, H:R]).then_inc(S.st_q1, 16)
+    g.sync.wait_ge(S.st_p0, 16)
+    g.sync.wait_ge(S.st_q0, 16)
+    g.scalar.wait_ge(S.st_p1, 16)
+    g.scalar.wait_ge(S.st_q1, 16)

@@ -4,30 +4,27 @@ from concourse.mybir import AluOpType
 D = 128
 R = 512
 H = R // 2
-BITS = 7
+NQ = R // D
+
+QP = [(0, 128, 5), (128, 256, 6), (256, 384, 7), (384, 448, 0), (448, 512, 1)]
 
 SCRATCH = {
+    "src": ("dram", [128, D], "bfloat16"),
     "land": ("sbuf", [128, 4 * D], "bfloat16"),
     "qs": ("sbuf", [128, R], "bfloat16"),
-    "ones": ("sbuf", [128, D], "bfloat16"),
-    "neg6": ("sbuf", [128, D], "bfloat16"),
-    "zero": ("sbuf", [128, D], "bfloat16"),
+    "ramp": ("sbuf", [128, D], "bfloat16"),
     "ident": ("sbuf", [128, D], "bfloat16"),
+    "xs": ("sbuf", [128, D], "bfloat16"),
     "s_bf": ("sbuf", [128, D], "bfloat16"),
     "p_bf": ("sbuf", [128, R], "bfloat16"),
     "q2_bf": ("sbuf", [128, R], "bfloat16"),
-    "ps_p0": ("psum", [128, 512], "float32"),
-    "ps_p1": ("psum", [128, 512], "float32"),
-    "ps_s": ("psum", [128, 512], "float32"),
-    "ps_q0": ("psum", [128, 512], "float32"),
-    "ps_q1": ("psum", [128, 512], "float32"),
-    "ps_c": ("psum", [128, 512], "float32"),
 }
-for _b in range(BITS):
-    SCRATCH["sg%d" % _b] = ("sbuf", [128, D >> (_b + 1), 2 << _b], "bfloat16")
-SEMAPHORES = ["ld_mt", "ld_q", "fill", "mm_c", "cp_id", "sent", "arr0", "arr1", "arr2", "arr3",
-              "mm_p0", "mm_p1", "mm_s", "mm_q0", "mm_q1", "cp_p0", "cp_p1", "cp_s", "cp_q0", "cp_q1",
-              "st_p0", "st_p1", "st_q0", "st_q1"]
+for _b in range(8):
+    SCRATCH["ps%d" % _b] = ("psum", [128, 512], "float32")
+SEMAPHORES = (["ld_src", "ld_q", "ld_own", "rdy", "cp_id", "sent", "arr0", "arr1", "arr2", "arr3", "ad_x",
+               "mm_s", "cp_s", "st_p0", "st_p1", "st_q0", "st_q1"]
+              + ["mm_p%d" % k for k in range(NQ)] + ["cp_p%d" % k for k in range(NQ)]
+              + ["mm_q%d" % k for k in range(len(QP))] + ["cp_q%d" % k for k in range(len(QP))])
 
 
 def _bits(mask):
@@ -43,20 +40,11 @@ def _mask(bits):
 
 def _plan(src, cores, topo):
     peers = [c for c in cores if c != src]
-    away = [c for c in peers if topo.chip(c) != topo.chip(src)]
-    near = [c for c in peers if topo.chip(c) == topo.chip(src)]
-    plan = {}
-    used = []
-    for k, c in enumerate(away):
-        e = _bits(topo.mask(src, c))
-        n = len(e) // len(away)
-        plan[c] = e[k * n:(k + 1) * n]
-        used += plan[c]
-    for c in near:
-        e = [b for b in _bits(topo.mask(src, c)) if b not in used]
-        plan[c] = e[:4]
-        used += plan[c]
-    return plan
+    away = sorted([c for c in peers if topo.chip(c) != topo.chip(src)], key=lambda c: topo.die(c) != topo.die(src))
+    near = [c for c in peers if topo.chip(c) == topo.chip(src)][0]
+    out = _bits(topo.mask(src, away[0]))
+    free = [b for b in _bits(topo.mask(src, near)) if b not in out]
+    return (away[0], near, away[1]), {away[0]: out, near: free[:8], away[1]: _bits(topo.mask(src, away[1]))}
 
 
 def rank_program(g, core, T, topo):
@@ -71,83 +59,98 @@ def rank_program(g, core, T, topo):
     def slot(j):
         return T.land[:, j * D:(j + 1) * D]
 
-    g.sync.dma_start(slot(rank), T.mt[:, :]).then_inc(S.ld_mt, 16)
-    g.sync.dma_start(T.qs[:, :], T.q[:, :]).then_inc(S.ld_q, 16)
+    def qq(k):
+        return T.qs[:, k * D:(k + 1) * D]
 
-    fills = 0
-    for b in range(BITS):
-        w = 1 << b
-        ve.memset(T["sg%d" % b][0:1, :, 0:w], -1.0).then_inc(S.fill, 1)
-        ve.memset(T["sg%d" % b][0:1, :, w:2 * w], 1.0).then_inc(S.fill, 1)
-        fills += 2
-    ve.memset(T.ones[0:1, :], 1.0).then_inc(S.fill, 1)
-    ve.memset(T.neg6[0:1, :], -6.0).then_inc(S.fill, 1)
-    ve.memset(T.zero[:, :], 0.0).then_inc(S.fill, 1)
-    fills += 3
-    te.wait_ge(S.fill, fills)
-    for b in range(BITS):
-        row = T["sg%d" % b][0:1, :, :]
-        te.matmul(T.ps_c[:, 0:D], row, row, b == 0, False).then_inc(S.mm_c, 1)
-    te.matmul(T.ps_c[:, 0:D], T.ones[0:1, :], T.neg6[0:1, :], False, True).then_inc(S.mm_c, 1)
-    ve.wait_ge(S.fill, fills)
-    ve.wait_ge(S.mm_c, BITS + 1)
-    ve.tensor_tensor(T.ident[:, :], T.ps_c[:, 0:D], T.zero[:, :], AluOpType.max).then_inc(S.cp_id, 1)
+    def bank(b, w):
+        return T["ps%d" % b][:, 0:w]
 
-    plan = _plan(core, cores, topo)
-    transfers = []
-    total = 0
-    for dst, eng in plan.items():
+    g.sync.dma_start(T.src[:, :], T.mt[:, :]).then_inc(S.ld_src, 16)
+    g.scalar.dma_start(T.qs[:, :], T.q[:, :]).then_inc(S.ld_q, 16)
+    g.sync.dma_start(slot(rank), T.mt[:, :]).then_inc(S.ld_own, 16)
+
+    g.iota(T.ramp[:, :], [[-1, D]], 0, 1, allow_small_or_imprecise_dtypes=True).then_inc(S.rdy, 1)
+    ve.wait_ge(S.rdy, 1)
+    ve.tensor_scalar(T.ident[:, :], T.ramp[:, :], 0.0, None, AluOpType.is_equal).then_inc(S.cp_id, 1)
+
+    (d1, dn, d2), eng = _plan(core, cores, topo)
+
+    def transfer(dst):
         rid, pid, _ = topo.addr(dst)
-        transfers.append(RemoteDMATransfer(dst_ids=[DstId(rid=rid, pnc=pid)], dma_engine_mask=_mask(eng),
-                                           remote_sem=S["arr%d" % rank], src=slot(rank), dst=slot(rank)))
-        total += len(eng)
-    g.wait_ge(S.ld_mt, 16)
-    g.remote_dma_fused(transfers, local_sem=S.sent)
-    g.wait_ge(S.sent, total)
+        return RemoteDMATransfer(dst_ids=[DstId(rid=rid, pnc=pid)], dma_engine_mask=_mask(eng[dst]),
+                                 remote_sem=S["arr%d" % rank], src=T.src[:, :], dst=slot(rank))
+    g.wait_ge(S.ld_src, 16)
+    g.remote_dma_fused([transfer(d1), transfer(dn)], local_sem=S.sent)
+    g.remote_dma_fused([transfer(d2)], local_sem=S.sent)
+    g.wait_ge(S.sent, len(eng[d1]) + len(eng[dn]) + len(eng[d2]))
 
-    def key(c):
-        return (c != core, topo.chip(c) != topo.chip(core), topo.die(c) != topo.die(core))
-    order = sorted(cores, key=key)
-    n = len(order)
-    te.wait_ge(S.ld_mt, 16)
+    cA = [c for c in cores if c != core and _plan(c, cores, topo)[0][0] == core][0]
+    cC = [c for c in cores if c != core and _plan(c, cores, topo)[0][1] == core][0]
+    cB = [c for c in cores if c != core and _plan(c, cores, topo)[0][2] == core][0]
+    jA, jC, jB = T.rank_of(cA), T.rank_of(cC), T.rank_of(cB)
+
+    def landed(queue, c):
+        queue.wait_ge(S["arr%d" % T.rank_of(c)], len(_plan(c, cores, topo)[1][core]))
+
+    def mm_p(k, lhsT, start, stop):
+        te.matmul(bank(k, D), lhsT, qq(k), start, stop).then_inc(S["mm_p%d" % k], 1)
+
+    def mm_s(lhsT, start, stop):
+        te.matmul(bank(4, D), lhsT, T.ident[:, :], start, stop).then_inc(S.mm_s, 1)
+
+    te.wait_ge(S.ld_own, 16)
     te.wait_ge(S.ld_q, 16)
-    for k, c in enumerate(order):
-        j = T.rank_of(c)
-        if c != core:
-            te.wait_ge(S["arr%d" % j], len(_plan(c, cores, topo)[core]))
-        a, z = k == 0, k == n - 1
-        te.matmul(T.ps_p0[:, 0:H], slot(j), T.qs[:, 0:H], a, z).then_inc(S.mm_p0, 1)
-        if k == 0:
-            te.matmul(T.ps_p1[:, 0:H], slot(j), T.qs[:, H:R], a, z).then_inc(S.mm_p1, 1)
-            te.wait_ge(S.cp_id, 1)
-            te.matmul(T.ps_s[:, 0:D], slot(j), T.ident[:, :], a, z).then_inc(S.mm_s, 1)
-        else:
-            te.matmul(T.ps_s[:, 0:D], slot(j), T.ident[:, :], a, z).then_inc(S.mm_s, 1)
-            te.matmul(T.ps_p1[:, 0:H], slot(j), T.qs[:, H:R], a, z).then_inc(S.mm_p1, 1)
-    te.wait_ge(S.cp_p0, 1)
+    for k in range(NQ):
+        mm_p(k, slot(rank), True, False)
+    te.wait_ge(S.cp_id, 1)
+    mm_s(slot(rank), True, False)
+    landed(te, cA)
+    mm_p(0, slot(jA), False, False)
+    mm_p(1, slot(jA), False, False)
+    landed(te, cC)
+    mm_p(0, slot(jC), False, False)
+    mm_p(1, slot(jC), False, False)
+    te.wait_ge(S.ad_x, 1)
+    mm_s(T.xs[:, :], False, False)
+    mm_p(2, T.xs[:, :], False, False)
+    mm_p(3, T.xs[:, :], False, False)
+    landed(te, cB)
+    mm_s(slot(jB), False, True)
+    for k in range(NQ):
+        mm_p(k, slot(jB), False, True)
     te.wait_ge(S.cp_s, 1)
-    te.matmul(T.ps_q0[:, 0:H], T.s_bf[:, :], T.p_bf[:, 0:H], True, True).then_inc(S.mm_q0, 1)
-    te.wait_ge(S.cp_p1, 1)
-    te.matmul(T.ps_q1[:, 0:H], T.s_bf[:, :], T.p_bf[:, H:R], True, True).then_inc(S.mm_q1, 1)
+    have = -1
+    for i, (lo, hi, b) in enumerate(QP):
+        while have < (hi - 1) // D:
+            have += 1
+            te.wait_ge(S["cp_p%d" % have], 1)
+        te.matmul(bank(b, hi - lo), T.s_bf[:, :], T.p_bf[:, lo:hi], True, True).then_inc(S["mm_q%d" % i], 1)
 
-    ve.wait_ge(S.mm_p0, n)
-    ve.tensor_copy(T.p_bf[:, 0:H], T.ps_p0[:, 0:H]).then_inc(S.cp_p0, 1)
-    ve.wait_ge(S.mm_s, n)
-    ve.tensor_copy(T.s_bf[:, :], T.ps_s[:, 0:D]).then_inc(S.cp_s, 1)
-    ve.wait_ge(S.mm_p1, n)
-    ve.tensor_copy(T.p_bf[:, H:R], T.ps_p1[:, 0:H]).then_inc(S.cp_p1, 1)
-    ve.wait_ge(S.mm_q0, 1)
-    ve.tensor_copy(T.q2_bf[:, 0:H], T.ps_q0[:, 0:H]).then_inc(S.cp_q0, 1)
-    ve.wait_ge(S.mm_q1, 1)
-    ve.tensor_copy(T.q2_bf[:, H:R], T.ps_q1[:, 0:H]).then_inc(S.cp_q1, 1)
+    landed(ve, cA)
+    landed(ve, cC)
+    ve.tensor_tensor(T.xs[:, :], slot(jA), slot(jC), AluOpType.add).then_inc(S.ad_x, 1)
+    ve.wait_ge(S.mm_s, 3)
+    ve.tensor_copy(T.s_bf[:, :], bank(4, D)).then_inc(S.cp_s, 1)
+    for k in range(NQ):
+        ve.wait_ge(S["mm_p%d" % k], 4 if k < 2 else 3)
+        ve.tensor_copy(T.p_bf[:, k * D:(k + 1) * D], bank(k, D)).then_inc(S["cp_p%d" % k], 1)
+    for i, (lo, hi, b) in enumerate(QP):
+        ve.wait_ge(S["mm_q%d" % i], 1)
+        ve.tensor_copy(T.q2_bf[:, lo:hi], bank(b, hi - lo)).then_inc(S["cp_q%d" % i], 1)
 
     g.sync.wait_ge(S.cp_p0, 1)
+    g.sync.wait_ge(S.cp_p1, 1)
     g.sync.dma_start(T.p[:, 0:H], T.p_bf[:, 0:H]).then_inc(S.st_p0, 16)
-    g.sync.wait_ge(S.cp_q0, 1)
-    g.sync.dma_start(T.q2[:, 0:H], T.q2_bf[:, 0:H]).then_inc(S.st_q0, 16)
-    g.scalar.wait_ge(S.cp_p1, 1)
+    g.scalar.wait_ge(S.cp_p2, 1)
+    g.scalar.wait_ge(S.cp_p3, 1)
     g.scalar.dma_start(T.p[:, H:R], T.p_bf[:, H:R]).then_inc(S.st_p1, 16)
-    g.scalar.wait_ge(S.cp_q1, 1)
+    for i, (lo, hi, b) in enumerate(QP):
+        if hi <= H:
+            g.sync.wait_ge(S["cp_q%d" % i], 1)
+    g.sync.dma_start(T.q2[:, 0:H], T.q2_bf[:, 0:H]).then_inc(S.st_q0, 16)
+    for i, (lo, hi, b) in enumerate(QP):
+        if hi > H:
+            g.scalar.wait_ge(S["cp_q%d" % i], 1)
     g.scalar.dma_start(T.q2[:, H:R], T.q2_bf[:, H:R]).then_inc(S.st_q1, 16)
     g.sync.wait_ge(S.st_p0, 16)
     g.sync.wait_ge(S.st_q0, 16)

from concourse.bass import DstId, RemoteDMATransfer
from concourse.mybir import AluOpType

D = 128
R = 512
H = R // 2
NQ = R // D

QP = [(0, 128, 5), (128, 256, 6), (256, 384, 7), (384, 448, 0), (448, 512, 1)]

SCRATCH = {
    "src": ("dram", [128, D], "bfloat16"),
    "land": ("sbuf", [128, 4 * D], "bfloat16"),
    "qs": ("sbuf", [128, R], "bfloat16"),
    "ramp": ("sbuf", [128, D], "bfloat16"),
    "ident": ("sbuf", [128, D], "bfloat16"),
    "xs": ("sbuf", [128, D], "bfloat16"),
    "s_bf": ("sbuf", [128, D], "bfloat16"),
    "p_bf": ("sbuf", [128, R], "bfloat16"),
    "q2_bf": ("sbuf", [128, R], "bfloat16"),
}
for _b in range(8):
    SCRATCH["ps%d" % _b] = ("psum", [128, 512], "float32")
SEMAPHORES = (["ld_src", "ld_q", "ld_own", "rdy", "cp_id", "sent", "arr0", "arr1", "arr2", "arr3", "ad_x",
               "mm_s", "cp_s", "st_p0", "st_p1", "st_q0", "st_q1"]
              + ["mm_p%d" % k for k in range(NQ)] + ["cp_p%d" % k for k in range(NQ)]
              + ["mm_q%d" % k for k in range(len(QP))] + ["cp_q%d" % k for k in range(len(QP))])


def _bits(mask):
    return [b for b in range(mask.bit_length()) if (mask >> b) & 1]


def _mask(bits):
    m = 0
    for b in bits:
        m |= 1 << b
    return m


def _plan(src, cores, topo):
    peers = [c for c in cores if c != src]
    away = sorted([c for c in peers if topo.chip(c) != topo.chip(src)], key=lambda c: topo.die(c) != topo.die(src))
    near = [c for c in peers if topo.chip(c) == topo.chip(src)][0]
    out = _bits(topo.mask(src, away[0]))
    free = [b for b in _bits(topo.mask(src, near)) if b not in out]
    return (away[0], near, away[1]), {away[0]: out, near: free[:8], away[1]: _bits(topo.mask(src, away[1]))}


def rank_program(g, core, T, topo):
    rank = T.rank_of(core)
    if rank is None:
        return
    S = T.sem
    cores = list(T.cores)
    te = g.tensor
    ve = g.vector

    def slot(j):
        return T.land[:, j * D:(j + 1) * D]

    def qq(k):
        return T.qs[:, k * D:(k + 1) * D]

    def bank(b, w):
        return T["ps%d" % b][:, 0:w]

    g.sync.dma_start(T.src[:, :], T.mt[:, :]).then_inc(S.ld_src, 16)
    g.scalar.dma_start(T.qs[:, :], T.q[:, :]).then_inc(S.ld_q, 16)
    g.sync.dma_start(slot(rank), T.mt[:, :]).then_inc(S.ld_own, 16)

    g.iota(T.ramp[:, :], [[-1, D]], 0, 1, allow_small_or_imprecise_dtypes=True).then_inc(S.rdy, 1)
    ve.wait_ge(S.rdy, 1)
    ve.tensor_scalar(T.ident[:, :], T.ramp[:, :], 0.0, None, AluOpType.is_equal).then_inc(S.cp_id, 1)

    (d1, dn, d2), eng = _plan(core, cores, topo)

    def transfer(dst):
        rid, pid, _ = topo.addr(dst)
        return RemoteDMATransfer(dst_ids=[DstId(rid=rid, pnc=pid)], dma_engine_mask=_mask(eng[dst]),
                                 remote_sem=S["arr%d" % rank], src=T.src[:, :], dst=slot(rank))
    g.wait_ge(S.ld_src, 16)
    g.remote_dma_fused([transfer(d1), transfer(dn)], local_sem=S.sent)
    g.remote_dma_fused([transfer(d2)], local_sem=S.sent)
    g.wait_ge(S.sent, len(eng[d1]) + len(eng[dn]) + len(eng[d2]))

    cA = [c for c in cores if c != core and _plan(c, cores, topo)[0][0] == core][0]
    cC = [c for c in cores if c != core and _plan(c, cores, topo)[0][1] == core][0]
    cB = [c for c in cores if c != core and _plan(c, cores, topo)[0][2] == core][0]
    jA, jC, jB = T.rank_of(cA), T.rank_of(cC), T.rank_of(cB)

    def landed(queue, c):
        queue.wait_ge(S["arr%d" % T.rank_of(c)], len(_plan(c, cores, topo)[1][core]))

    def mm_p(k, lhsT, start, stop):
        te.matmul(bank(k, D), lhsT, qq(k), start, stop).then_inc(S["mm_p%d" % k], 1)

    def mm_s(lhsT, start, stop):
        te.matmul(bank(4, D), lhsT, T.ident[:, :], start, stop).then_inc(S.mm_s, 1)

    te.wait_ge(S.ld_own, 16)
    te.wait_ge(S.ld_q, 16)
    for k in range(NQ):
        mm_p(k, slot(rank), True, False)
    te.wait_ge(S.cp_id, 1)
    mm_s(slot(rank), True, False)
    landed(te, cA)
    mm_p(0, slot(jA), False, False)
    mm_p(1, slot(jA), False, False)
    landed(te, cC)
    mm_p(0, slot(jC), False, False)
    mm_p(1, slot(jC), False, False)
    te.wait_ge(S.ad_x, 1)
    mm_s(T.xs[:, :], False, False)
    mm_p(2, T.xs[:, :], False, False)
    mm_p(3, T.xs[:, :], False, False)
    landed(te, cB)
    mm_s(slot(jB), False, True)
    for k in range(NQ):
        mm_p(k, slot(jB), False, True)
    te.wait_ge(S.cp_s, 1)
    have = -1
    for i, (lo, hi, b) in enumerate(QP):
        while have < (hi - 1) // D:
            have += 1
            te.wait_ge(S["cp_p%d" % have], 1)
        te.matmul(bank(b, hi - lo), T.s_bf[:, :], T.p_bf[:, lo:hi], True, True).then_inc(S["mm_q%d" % i], 1)

    landed(ve, cA)
    landed(ve, cC)
    ve.tensor_tensor(T.xs[:, :], slot(jA), slot(jC), AluOpType.add).then_inc(S.ad_x, 1)
    ve.wait_ge(S.mm_s, 3)
    ve.tensor_copy(T.s_bf[:, :], bank(4, D)).then_inc(S.cp_s, 1)
    for k in range(NQ):
        ve.wait_ge(S["mm_p%d" % k], 4 if k < 2 else 3)
        ve.tensor_copy(T.p_bf[:, k * D:(k + 1) * D], bank(k, D)).then_inc(S["cp_p%d" % k], 1)
    for i, (lo, hi, b) in enumerate(QP):
        ve.wait_ge(S["mm_q%d" % i], 1)
        ve.tensor_copy(T.q2_bf[:, lo:hi], bank(b, hi - lo)).then_inc(S["cp_q%d" % i], 1)

    g.sync.wait_ge(S.cp_p0, 1)
    g.sync.wait_ge(S.cp_p1, 1)
    g.sync.dma_start(T.p[:, 0:H], T.p_bf[:, 0:H]).then_inc(S.st_p0, 16)
    g.scalar.wait_ge(S.cp_p2, 1)
    g.scalar.wait_ge(S.cp_p3, 1)
    g.scalar.dma_start(T.p[:, H:R], T.p_bf[:, H:R]).then_inc(S.st_p1, 16)
    for i, (lo, hi, b) in enumerate(QP):
        if hi <= H:
            g.sync.wait_ge(S["cp_q%d" % i], 1)
    g.sync.dma_start(T.q2[:, 0:H], T.q2_bf[:, 0:H]).then_inc(S.st_q0, 16)
    for i, (lo, hi, b) in enumerate(QP):
        if hi > H:
            g.scalar.wait_ge(S["cp_q%d" % i], 1)
    g.scalar.dma_start(T.q2[:, H:R], T.q2_bf[:, H:R]).then_inc(S.st_q1, 16)
    g.sync.wait_ge(S.st_p0, 16)
    g.sync.wait_ge(S.st_q0, 16)
    g.scalar.wait_ge(S.st_p1, 16)
    g.scalar.wait_ge(S.st_q1, 16)
